import numpy as np
import ml_dtypes


def mxq(x, axis, fmt="e4m3"):
    dtype, down = {"e4m3": (ml_dtypes.float8_e4m3fn, 7), "e5m2": (ml_dtypes.float8_e5m2, 14)}[fmt]
    v = np.moveaxis(np.asarray(x, np.float32).astype(ml_dtypes.bfloat16).astype(np.float64), axis, -1)
    blocks = v.reshape(v.shape[:-1] + (-1, 32))
    amax = np.abs(blocks).max(-1, keepdims=True)
    byte = np.maximum(np.where(amax > 0, np.frexp(amax)[1] - 1 + 127, 0) - down, 1)
    scale = np.exp2(byte - 127.0)
    codes = (blocks / scale).astype(np.float32).astype(dtype).astype(np.float64)
    return np.moveaxis((codes * scale).reshape(v.shape), -1, axis)


WIDE = False


def mx_kscale(k):
    if not WIDE:
        return np.ones(k)
    levels = np.array([10, -10, 5, -5, 0])
    if k % 512:
        return np.exp2(np.random.permutation(np.resize(levels, k // 32))).repeat(32)
    a = np.empty((k // 512, 16))
    for p in range(k // 512):
        a[p, :8] = np.random.permutation(np.resize(levels, 8))
        for g in range(8):
            far = levels[np.abs(levels - a[p, g]) >= 10]
            a[p, g + 8] = far[np.random.randint(len(far))]
    return np.exp2(a.ravel()).repeat(32)


def f64(x):
    return np.asarray(x).astype(np.float64)


def striped(idx):
    return np.tile(idx.reshape(-1, 16).T, (8, 1)).astype(np.uint16)


def unstriped(offs):
    return offs[:16].T.reshape(-1).astype(np.int64)


E2M1 = np.array([0.0, 0.5, 1.0, 1.5, 2.0, 3.0, 4.0, 6.0, -0.0, -0.5, -1.0, -1.5, -2.0, -3.0, -4.0, -6.0])


def pack_weight(w, fmt):
    k, n = w.shape
    w = f64(np.asarray(w, np.float32).astype(ml_dtypes.bfloat16)).reshape(k // 32, 32, n)
    amax = np.abs(w).max(1)
    if fmt == "e4m3":
        byte = np.frexp(amax)[1] - 1 + 127 - 7
    else:
        mant, ex = np.frexp(amax / 6.0)
        byte = np.where(mant > 0.5, ex, ex - 1) + 127
    byte = np.clip(np.where(amax > 0, byte, 1), 1, 254)
    scaled = (w * np.exp2(127.0 - byte)[:, None, :]).reshape(k, n).astype(np.float32)
    by_word = np.ascontiguousarray(scaled.reshape(k // 512, 128, 4, n).transpose(0, 1, 3, 2))
    if fmt == "e4m3":
        words = by_word.astype(ml_dtypes.float8_e4m3fn).view(np.uint8)
    else:
        c = by_word.astype(ml_dtypes.float4_e2m1fn).view(np.uint8) & 0xF
        words = (c[..., 0::2] | (c[..., 1::2] << 4)).reshape(k // 512, 128, 2 * n)
    return np.ascontiguousarray(words), np.ascontiguousarray(byte.astype(np.uint8).reshape(k // 512, 16, n))


def unpack_weight(words, scales, fmt):
    g, _, n = scales.shape
    words = np.ascontiguousarray(words).reshape(g, 128, n, -1)
    if fmt == "e4m3":
        vals = words.view(ml_dtypes.float8_e4m3fn).astype(np.float64)
    else:
        nib = np.empty((g, 128, n, 4), np.uint8)
        nib[..., 0::2] = words & 0xF
        nib[..., 1::2] = words >> 4
        vals = E2M1[nib]
    vals = vals * np.repeat(np.exp2(scales.astype(np.float64) - 127.0), 8, axis=1)[..., None]
    return vals.transpose(0, 1, 3, 2).reshape(g * 512, n)


def gelu(v):
    return 0.5 * v * (1.0 + np.tanh(np.sqrt(2.0 / np.pi) * (v + 0.044715 * v**3)))


def twice(P):
    return np.random.permutation(np.repeat(np.arange(P), 2))


def bf(x):
    return np.asarray(x, np.float32).astype(ml_dtypes.bfloat16)


def planes(Y):
    n, m = Y.shape
    b = f64(bf(Y)).reshape(n // 32, 32, m)
    amax = np.abs(b).max(1)
    byte = np.clip(np.where(amax > 0, np.frexp(amax)[1] - 1 + 127 - 7, 1), 1, 254)
    codes = (b * np.exp2(127.0 - byte)[:, None, :]).reshape(n, m).astype(np.float32).astype(ml_dtypes.float8_e4m3fn).view(np.uint8)
    words = codes.reshape(n // 512, 128, 4, m).transpose(0, 1, 3, 2)
    return np.ascontiguousarray(words), np.ascontiguousarray(byte.astype(np.uint8).reshape(n // 512, 16, m))


K, H, T, S, P = 512, 1024, 4096, 1024, 512

def setup_inputs():
    n = np.random.standard_normal
    s = mx_kscale(K)[:, None]
    u = mx_kscale(H)[:, None]
    d = {}
    d["tab_words"], d["tab_scales"] = pack_weight(n((K, T)) * s, "e4m3")
    d["offs"] = striped(np.random.permutation(T)[:S])
    d["pos1"] = striped(np.random.permutation(S)[:P])
    d["pos2"] = striped(np.random.permutation(S)[:P])
    d["pos3"] = striped(twice(P))
    d["wa"] = (n((K, H)) / s * u.T / K ** 0.5).astype(np.float32)
    d["wb_words"], d["wb_scales"] = pack_weight(n((K, H)) / s * u.T / K ** 0.5, "e2m1")
    d["wc"] = (0.8 * n((K, H)) / s * u.T / K ** 0.5).astype(np.float32)
    d["wd"] = (0.7 * n((H, H)) / u / H ** 0.5).astype(np.float32)
    d["gh"] = (np.random.uniform(0.5, 1.0, H) / u[:, 0]).astype(np.float32)
    d["gn"] = np.exp(0.8 * n(H)).astype(np.float32)
    return d

def reference(tab_words, tab_scales, offs, pos1, pos2, pos3, wa, wb_words, wb_scales, wc, wd, gh, gn):
    v = unpack_weight(tab_words, tab_scales, "e4m3")[:, unstriped(offs)]
    a = mxq(f64(wa), 0, "e4m3").T @ v
    b = unpack_weight(wb_words, wb_scales, "e2m1").T @ v
    c = mxq(f64(wc), 0, "e4m3").T @ v
    h = np.minimum(a, b) + c
    x = h[:, unstriped(pos1)] - h[:, unstriped(pos2)]
    trolley = mxq(f64(wd), 0, "e4m3").T @ mxq(x, 0, "e4m3")
    raised = trolley[:, unstriped(pos3)]
    y = f64(gn)[:, None] * np.tanh(raised + f64(gh)[:, None] * h)
    words, scales = planes(y)
    return y, words, scales

from contextlib import ExitStack

import concourse.mybir as mybir

F32 = mybir.dt.float32
BF16 = mybir.dt.bfloat16
I32 = mybir.dt.int32
U32 = mybir.dt.uint32
U16 = mybir.dt.uint16
U8 = mybir.dt.uint8
FP8X4 = mybir.dt.float8_e4m3fn_x4
FP4X4 = mybir.dt.float4_e2m1fn_x4
ALU = mybir.AluOpType
ACT = mybir.ActivationFunctionType

K, H, T, S, M = 512, 1024, 4096, 1024, 512
P = 128
PACK = 4
GROUP = P * PACK
N = 512
SPARE = 16
FOLDED = 3
FLOPS = 2 * (3 * K * H * S + H * H * M)
BYTES = 4 * (2 * K * H + H * H + 2 * H + H * S) + K * T + 16 * T + K * H // 2 + 16 * H + H * S + 32 * S


def tile_list_pasta_crack_features_kernel(
    tc, tab_words, tab_scales, offs, pos1, pos2, pos3, wa, wb_words, wb_scales, wc, wd, gh, gn, out_0, out_1, out_2
):
    nc = tc.nc
    with ExitStack() as ctx:
        keep = ctx.enter_context(tc.tile_pool(name="keep", bufs=1))
        ring = ctx.enter_context(tc.tile_pool(name="ring", bufs=1))
        psum = ctx.enter_context(tc.psum_pool(name="psum", bufs=2))

        def load_scale_rows(plane, rows):
            for q in range(4):
                nc.scalar.dma_start(
                    out=plane[32 * q : 32 * q + 4, :].bitcast(I32), in_=rows[4 * q : 4 * q + 4, :].bitcast(I32)
                )

        def load_list(name, source):
            tile = keep.tile(list(source.shape), U16, name=name)
            nc.sync.dma_start(tile[:], source)
            return tile

        def load_rows(weight, g_row, g_col):
            raw = ring.tile([P, PACK, GROUP], F32, name="four", tag="four", bufs=8, align_bytes=64)
            block = weight[g_row * GROUP : (g_row + 1) * GROUP, g_col * GROUP : (g_col + 1) * GROUP]
            nc.sync.dma_start(out=raw[:], in_=block.rearrange("(p j) c -> p j c", j=PACK))
            return raw

        def load_vector(name, vec):
            tile = keep.tile([P, H // GROUP, PACK], F32, name=name)
            nc.sync.dma_start(out=tile[:], in_=vec.rearrange("(g p t) -> p g t", p=P, t=PACK))
            return tile

        def woven_tile():
            return ring.tile([P, PACK * GROUP], BF16, name="woven", tag="woven", bufs=3, align_bytes=64)

        def deal_weight(raw, vector_m):
            woven = woven_tile()
            dst = woven[:].rearrange("p (t m j) -> p m j t", t=PACK, j=PACK)
            src = raw[:].rearrange("p j (m t) -> p m j t", t=PACK)
            if vector_m > 0:
                nc.vector.tensor_copy(out=dst[:, :vector_m], in_=src[:, :vector_m])
            if vector_m < P:
                nc.scalar.copy(out=dst[:, vector_m:], in_=src[:, vector_m:])
            return woven

        def weave(four, vector_c, width=N):
            woven = woven_tile()[:, : PACK * width]
            dst = woven.rearrange("p (c i t) -> p c t i", i=4, t=PACK)
            src = four[:, :, :width].rearrange("p t (c i) -> p c t i", i=4)
            if vector_c > 0:
                nc.vector.tensor_copy(out=dst[:, :vector_c], in_=src[:, :vector_c])
            if vector_c < width // 4:
                nc.scalar.copy(out=dst[:, vector_c:], in_=src[:, vector_c:])
            return woven

        def quantize(name, woven):
            codes = keep.tile([P, N], U32, name=name + "_codes", align_bytes=64)
            scales = keep.tile([P, N], U8, name=name + "_scales", align_bytes=64)
            nc.vector.quantize_mx(out=codes[:].bitcast(FP8X4), scales=scales[:], in_=woven[:, :])
            return codes, scales

        table_scales = keep.tile([P, T], U8, name="table_scales", align_bytes=64)
        wb_raw_scales = keep.tile([P, H], U8, name="wb_raw_scales", align_bytes=64)
        nc.vector.memset(table_scales[:].bitcast(I32), 0)
        nc.gpsimd.memset(wb_raw_scales[:].bitcast(I32), 0)
        offs_t = load_list("offs_t", offs)
        load_scale_rows(table_scales, tab_scales[0])
        load_scale_rows(wb_raw_scales, wb_scales[0])
        wb_raw = keep.tile([P, 2 * H], U8, name="wb_raw", align_bytes=64)
        nc.sync.dma_start(out=wb_raw[:].bitcast(I32), in_=wb_words[0].bitcast(I32))
        table = keep.tile([P, T], U32, name="table", align_bytes=64)
        nc.sync.dma_start(out=table[:].bitcast(I32), in_=tab_words[0].rearrange("p n i -> p (n i)").bitcast(I32))
        wa_raw = [load_rows(wa, 0, 0)]
        wc_raw = [load_rows(wc, 0, 0)]
        pos2_t = load_list("pos2_t", pos2)
        pos1_t = load_list("pos1_t", pos1)
        gh_t = load_vector("gh_t", gh)
        wa_raw.append(load_rows(wa, 0, 1))
        wc_raw.append(load_rows(wc, 0, 1))
        wd_raw = [load_rows(wd, u % 2, u // 2) for u in range(4)]
        pos3_t = load_list("pos3_t", pos3)
        gn_t = load_vector("gn_t", gn)

        trolley = [keep.tile([P, M + SPARE], F32, name="trolley%d" % i) for i in range(8)]
        for i in range(8):
            nc.gpsimd.memset(trolley[i][:, M:], 0.0)

        v_scales = keep.tile([P, S], U8, name="v_scales", align_bytes=64)
        v_words = keep.tile([P, S], U32, name="v_words", align_bytes=64)
        nc.vector.tensor_copy(out=v_scales[:], in_=table_scales[:].indirect(offs_t[:]))
        wb_dealt = keep.tile([P, 2 * H], U8, name="wb_dealt", align_bytes=64)
        wb_dealt_scales = keep.tile([P, H], U8, name="wb_dealt_scales", align_bytes=64)
        nc.vector.tensor_copy(
            out=wb_dealt[:].rearrange("p (g t m b) -> p g m t b", g=2, t=PACK, b=2),
            in_=wb_raw[:].rearrange("p (g m t b) -> p g m t b", g=2, t=PACK, b=2),
        )
        nc.vector.tensor_copy(
            out=wb_dealt_scales[:].rearrange("p (g t m) -> p g m t", g=2, t=PACK),
            in_=wb_raw_scales[:].rearrange("p (g m t) -> p g m t", g=2, t=PACK),
        )
        for half in range(2):
            nc.vector.tensor_copy(
                out=v_words[:, half * N : (half + 1) * N],
                in_=table[:].indirect(offs_t[:, half * 32 : (half + 1) * 32]),
            )

        wa_q = [quantize("wa0", deal_weight(wa_raw[0], 84))]
        wc_q = [quantize("wc0", deal_weight(wc_raw[0], 64))]
        wd_q = []
        x_q = []

        def product(tag, weights, half):
            bank = psum.tile([P, N], F32, name=tag, tag=tag)
            cols = slice(half * N, (half + 1) * N)
            for n, (codes, scales) in enumerate(weights):
                nc.tensor.matmul_mx(
                    out=bank[:], lhsT=codes, lhsT_scale=scales,
                    rhs=v_words[:, cols].bitcast(FP8X4), rhs_scale=v_scales[:, cols],
                    start=(n == 0), stop=(n == len(weights) - 1),
                )
            return bank

        h_scaled = [keep.tile([P, S], F32, name="h_scaled%d" % i) for i in range(8)]
        h = {}
        lower = {}
        x_four = {}
        woven_w = {}

        def pick_lower(i):
            lower[i] = ring.tile([P, M], F32, name="lower", tag="lower", bufs=2)
            nc.vector.tensor_copy(out=lower[i][:], in_=h[i][:].indirect(pos2_t[:]))

        def pick_upper(i):
            g, t = divmod(i, PACK)
            if t == 0:
                x_four[g] = ring.tile([P, PACK, M], F32, name="four", tag="four", bufs=8, align_bytes=64)
            nc.vector.tensor_tensor(x_four[g][:, t, :], h[i][:].indirect(pos1_t[:]), lower[i][:], ALU.subtract)
            nc.scalar.activation(h_scaled[i][:], h[i][:], ACT.Copy, scale=gh_t[:, g, t : t + 1])

        later = {0: ("wa1", wa_raw[1], wa_q), 1: ("wc1", wc_raw[1], wc_q)}
        for u in range(4):
            later[3 + u] = ("wd%d" % u, wd_raw[u], wd_q)

        for i in range(8):
            g, t = divmod(i, PACK)
            cols = slice(t * P, (t + 1) * P)
            w_a = (wa_q[g][0][:, cols].bitcast(FP8X4), wa_q[g][1][:, cols])
            w_b = (wb_dealt[:, 2 * i * P : 2 * (i + 1) * P].bitcast(FP4X4), wb_dealt_scales[:, i * P : (i + 1) * P])
            w_c = (wc_q[g][0][:, cols].bitcast(FP8X4), wc_q[g][1][:, cols])
            folded = i >= 8 - FOLDED
            h[i] = ring.tile([P, S], F32, name="h", tag="h", bufs=3)
            least = []
            b_banks = []
            a_sbs = []
            for half in range(2):
                a_bank = product("a", [w_a, w_c] if folded else [w_a], half)
                b_banks.append(product("b", [w_b, w_c] if folded else [w_b], half))
                a_sb = ring.tile([P, N], F32, name="left", tag="left", bufs=3)
                nc.scalar.copy(out=a_sb[:], in_=a_bank[:])
                a_sbs.append(a_sb)
            if folded:
                pick_lower(i - 1)
                for half in range(2):
                    nc.vector.tensor_tensor(h[i][:, half * N : (half + 1) * N], b_banks[half][:], a_sbs[half][:], ALU.min)
            else:
                c_banks = [product("c", [w_c], half) for half in range(2)]
                for half in range(2):
                    m = ring.tile([P, N], F32, name="right", tag="right", bufs=4)
                    nc.vector.tensor_tensor(m[:], b_banks[half][:], a_sbs[half][:], ALU.min)
                    least.append(m)
                if i > 0:
                    pick_lower(i - 1)
                for half in range(2):
                    nc.vector.tensor_tensor(h[i][:, half * N : (half + 1) * N], c_banks[half][:], least[half][:], ALU.add)
            if i > 0:
                pick_upper(i - 1)
            if i - 1 in later:
                name, raw, done = later[i - 1]
                done.append(quantize(name, woven_w[i - 1]))
            if i in later:
                woven_w[i] = deal_weight(later[i][1], 0)
            if i == PACK + 1:
                x_q.append(quantize("x0", woven_x))
            if i == PACK:
                woven_x = weave(x_four[0], 0)
        pick_lower(7)
        pick_upper(7)
        x_q.append(quantize("x1", weave(x_four[1], 84)))

        for i in range(8):
            g, t = divmod(i, PACK)
            cols = slice(t * P, (t + 1) * P)
            bank = psum.tile([P, N], F32, name="d", tag="d")
            for gk in range(2):
                codes, scales = wd_q[2 * g + gk]
                nc.tensor.matmul_mx(
                    out=bank[:], lhsT=codes[:, cols].bitcast(FP8X4), lhsT_scale=scales[:, cols],
                    rhs=x_q[gk][0][:].bitcast(FP8X4), rhs_scale=x_q[gk][1][:], start=(gk == 0), stop=(gk == 1),
                )
            nc.scalar.copy(out=trolley[i][:, :M], in_=bank[:])

        y_rows = out_0.rearrange("(g p t) j -> g p t j", p=P, t=PACK)
        y_scales = [keep.tile([P, S], U8, name="y_scales%d" % g, align_bytes=64) for g in range(2)]
        y_four = {}

        units = [(0, 0, 512, 64), (0, 512, 512, 64), (1, 0, 512, 64), (1, 512, 256, 40), (1, 768, 256, 64)]

        def finish(u):
            g, start, width, vector_c = units[u]
            cols = slice(start, start + width)
            woven = weave(y_four[u], vector_c, width)
            codes = keep.tile([P, width], U32, name="y_codes%d" % u, align_bytes=64)
            nc.vector.quantize_mx(out=codes[:].bitcast(FP8X4), scales=y_scales[g][:, cols], in_=woven)
            words = out_1[g].rearrange("p m i -> p (m i)").bitcast(I32)
            nc.sync.dma_start(out=words[:, cols], in_=codes[:].bitcast(I32))
            if start + width == S:
                for q in range(4):
                    queue = nc.sync if q % 2 == 0 else nc.scalar
                    queue.dma_start(
                        out=out_2[g][4 * q : 4 * q + 4, :].bitcast(I32),
                        in_=y_scales[g][32 * q : 32 * q + 4, :].bitcast(I32),
                    )

        for u, (g, start, width, vector_c) in enumerate(units):
            cols = slice(start, start + width)
            y_four[u] = ring.tile([P, PACK, N], F32, name="four", tag="four", bufs=8, align_bytes=64)
            for t in range(PACK):
                i = g * PACK + t
                z = ring.tile([P, N], F32, name="right", tag="right", bufs=4)
                nc.vector.tensor_tensor(
                    z[:, :width], trolley[i][:].indirect(pos3_t[:, start // 16 : (start + width) // 16]),
                    h_scaled[i][:, cols], ALU.add,
                )
                bent = ring.tile([P, N], F32, name="left", tag="left", bufs=3)
                nc.scalar.activation(bent[:, :width], z[:, :width], ACT.Tanh)
                nc.scalar.activation(y_four[u][:, t, :width], bent[:, :width], ACT.Copy, scale=gn_t[:, g, t : t + 1])
                nc.sync.dma_start(out=y_rows[g][:, t, cols], in_=y_four[u][:, t, :width])
                if t == 1 and u > 0:
                    finish(u - 1)
        finish(len(units) - 1)
